import numpy as np
import ml_dtypes


def mxq(x, axis, fmt="e4m3"):
    dtype, down = {"e4m3": (ml_dtypes.float8_e4m3fn, 7), "e5m2": (ml_dtypes.float8_e5m2, 14)}[fmt]
    v = np.moveaxis(np.asarray(x, np.float32).astype(ml_dtypes.bfloat16).astype(np.float64), axis, -1)
    blocks = v.reshape(v.shape[:-1] + (-1, 32))
    amax = np.abs(blocks).max(-1, keepdims=True)
    byte = np.maximum(np.where(amax > 0, np.frexp(amax)[1] - 1 + 127, 0) - down, 1)
    scale = np.exp2(byte - 127.0)
    codes = (blocks / scale).astype(np.float32).astype(dtype).astype(np.float64)
    return np.moveaxis((codes * scale).reshape(v.shape), -1, axis)


WIDE = False


def mx_kscale(k):
    if not WIDE:
        return np.ones(k)
    levels = np.array([10, -10, 5, -5, 0])
    if k % 512:
        return np.exp2(np.random.permutation(np.resize(levels, k // 32))).repeat(32)
    a = np.empty((k // 512, 16))
    for p in range(k // 512):
        a[p, :8] = np.random.permutation(np.resize(levels, 8))
        for g in range(8):
            far = levels[np.abs(levels - a[p, g]) >= 10]
            a[p, g + 8] = far[np.random.randint(len(far))]
    return np.exp2(a.ravel()).repeat(32)


def f64(x):
    return np.asarray(x).astype(np.float64)


def striped(idx):
    return np.tile(np.asarray(idx).reshape(-1, 16).T, (8, 1)).astype(np.uint16)


def unstriped(offs):
    return offs[:16].T.reshape(-1).astype(np.int64)


E2M1 = np.array([0.0, 0.5, 1.0, 1.5, 2.0, 3.0, 4.0, 6.0, -0.0, -0.5, -1.0, -1.5, -2.0, -3.0, -4.0, -6.0])


def pack_weight(w, fmt):
    k, n = w.shape
    w = f64(np.asarray(w, np.float32).astype(ml_dtypes.bfloat16)).reshape(k // 32, 32, n)
    amax = np.abs(w).max(1)
    if fmt == "e4m3":
        byte = np.frexp(amax)[1] - 1 + 127 - 7
    else:
        mant, ex = np.frexp(amax / 6.0)
        byte = np.where(mant > 0.5, ex, ex - 1) + 127
    byte = np.clip(np.where(amax > 0, byte, 1), 1, 254)
    scaled = (w * np.exp2(127.0 - byte)[:, None, :]).reshape(k, n).astype(np.float32)
    by_word = np.ascontiguousarray(scaled.reshape(k // 512, 128, 4, n).transpose(0, 1, 3, 2))
    if fmt == "e4m3":
        words = by_word.astype(ml_dtypes.float8_e4m3fn).view(np.uint8)
    else:
        c = by_word.astype(ml_dtypes.float4_e2m1fn).view(np.uint8) & 0xF
        words = (c[..., 0::2] | (c[..., 1::2] << 4)).reshape(k // 512, 128, 2 * n)
    return np.ascontiguousarray(words), np.ascontiguousarray(byte.astype(np.uint8).reshape(k // 512, 16, n))


def unpack_weight(words, scales, fmt):
    g, _, n = scales.shape
    words = np.ascontiguousarray(words).reshape(g, 128, n, -1)
    if fmt == "e4m3":
        vals = words.view(ml_dtypes.float8_e4m3fn).astype(np.float64)
    else:
        nib = np.empty((g, 128, n, 4), np.uint8)
        nib[..., 0::2] = words & 0xF
        nib[..., 1::2] = words >> 4
        vals = E2M1[nib]
    vals = vals * np.repeat(np.exp2(scales.astype(np.float64) - 127.0), 8, axis=1)[..., None]
    return vals.transpose(0, 1, 3, 2).reshape(g * 512, n)


def softplus(v):
    return np.log(1.0 + np.exp(v))


def sigmoid(v):
    return 1.0 / (1.0 + np.exp(-v))


D, K, R, T, I, Q, G = 512, 512, 512, 2048, 512, 128, 64


def setup_inputs():
    n = np.random.standard_normal
    idx = np.random.permutation(T)[:I]
    fd = mx_kscale(D)
    fk = mx_kscale(K)
    fr = mx_kscale(R)
    keysp = pack_weight(n((D, T)) / fd[:, None], "e2m1")
    tabp = pack_weight(n((K, T)) / fk[:, None], "e2m1")
    return {
        "query": (n((D, Q)) * 0.9 / np.sqrt(D) * fd[:, None]).astype(np.float32),
        "keys_words": keysp[0],
        "keys_scales": keysp[1],
        "th": (np.random.uniform(-0.3, 0.6, (Q, 1))).astype(np.float32),
        "reserve": (np.random.uniform(50.0, 200.0, (Q, 1))).astype(np.float32),
        "tab_words": tabp[0],
        "tab_scales": tabp[1],
        "w1": (n((K, R)) * 1 / np.sqrt(K) * fk[:, None]).astype(np.float32),
        "temper": (np.random.uniform(0.4, 1.0, (R, 1))).astype(np.float32),
        "gout": (n((R, Q)) * 1 / np.sqrt(R) * fr[:, None]).astype(np.float32),
        "hsc": (np.random.uniform(0.7, 1.4, (R, 1)) / fr[:, None]).astype(np.float32),
        "old": (0.5 * n((Q, T))).astype(np.float32),
        "offs": striped(idx),
    }


def reference(query, keys_words, keys_scales, th, reserve, tab_words, tab_scales, w1, temper, gout, hsc, old, offs):
    idx = unstriped(offs)
    keysu = unpack_weight(keys_words, keys_scales, "e2m1")
    tabu = unpack_weight(tab_words, tab_scales, "e2m1")
    queryq = mxq(f64(query), 0, "e4m3")
    keysidxg = keysu[:, idx]
    a = queryq.T @ keysidxg
    p = softplus(a - f64(th))
    z = np.sum(p, axis=1, keepdims=True) + f64(reserve)
    w1q = mxq(f64(w1), 0, "e4m3")
    tabidxg = tabu[:, idx]
    zh = w1q.T @ tabidxg
    ht = np.exp(zh * f64(temper))
    mz = ht.reshape(R, G, I // G).sum(axis=2)
    mzr = np.repeat(mz, I // G, axis=1)
    hv = ht / mzr * 4.0
    hs1 = hv * f64(hsc)
    goutq = mxq(f64(gout), 0, "e4m3")
    hs1q = mxq(hs1, 0, "e4m3")
    c0 = goutq.T @ hs1q
    dz = np.sum(c0 * p / np.square(z) * (-1.0), axis=1, keepdims=True)
    dp = c0 / z + dz
    da = dp * sigmoid(a - f64(th))
    gs = da * 512.0
    gf = np.zeros((Q, T))
    gf[:, idx] = gs
    y = f64(old) + gf
    return y

@@ -1,0 +1,240 @@
+from contextlib import ExitStack
+
+import concourse.mybir as mybir
+from concourse.masks import make_identity
+
+D, K, R, T, I, Q, G = 512, 512, 512, 2048, 512, 128, 64
+FLOPS = 2 * (D * Q * I + K * R * I + R * Q * I)
+
+F32 = mybir.dt.float32
+BF16 = mybir.dt.bfloat16
+I32 = mybir.dt.int32
+U32 = mybir.dt.uint32
+U16 = mybir.dt.uint16
+U8 = mybir.dt.uint8
+FP8X4 = mybir.dt.float8_e4m3fn_x4
+FP4X4 = mybir.dt.float4_e2m1fn_x4
+ALU = mybir.AluOpType
+ACT = mybir.ActivationFunctionType
+
+P = 128
+PACK = 4
+GROUP = I // G
+CHUNKS = 2
+CH = I // CHUNKS
+LINE = 4
+HALF = R // 2
+STORE = (256, 512, 512, 512, 256)
+
+
+def tile_attend_blrshared_capped_kernel(tc, query, keys_words, keys_scales, th, reserve, tab_words, tab_scales,
+                                         w1, temper, gout, hsc, old, offs, out):
+    nc = tc.nc
+    with ExitStack() as ctx:
+        sb = ctx.enter_context(tc.tile_pool(name="sb", bufs=1))
+        ps = ctx.enter_context(tc.psum_pool(name="ps", bufs=1))
+
+        def tile(name, shape, dtype):
+            return sb.tile(shape, dtype, name=name, align_bytes=64)
+
+        def bank(name, tag, cols):
+            return ps.tile([P, cols], F32, name=name, tag=tag)
+
+        offsets = sb.tile([P, I // 16], U16, name="offsets")
+        nc.sync.dma_start(offsets[:], offs)
+
+        def load_scales(name, src, queue):
+            win = tile(name, [P, T], U8)
+            nc.vector.memset(win[:].bitcast(I32), 0)
+            rows = src[0].bitcast(I32).rearrange("(a r) c -> r a c", r=4)
+            for r in range(4):
+                queue.dma_start(win[r:P:32, :].bitcast(I32), rows[r])
+            return win
+
+        def load_words(name, src):
+            win = tile(name, [P, T], U16)
+            nc.sync.dma_start(win[:].bitcast(I32), src[0].bitcast(I32))
+            return win
+
+        def load_rows(name, src, cols):
+            raw = tile(name, [P, PACK, cols.stop - cols.start], F32)
+            nc.sync.dma_start(raw[:], src.rearrange("(p j) c -> p j c", j=PACK)[:, :, cols])
+            return raw
+
+        def load_vec(name, src, queue):
+            n = src.shape[0] // P
+            vec = tile(name, [P, n], F32)
+            queue.dma_start(vec[:], src.rearrange("(p t) o -> p (t o)", t=n))
+            return vec
+
+        w_raw = [load_rows("w_raw0", w1, slice(0, HALF))]
+        tab_s = load_scales("tab_s", tab_scales, nc.sync)
+        w_raw.append(load_rows("w_raw1", w1, slice(HALF, R)))
+        tab_w = load_words("tab_w", tab_words)
+        gf = tile("gf", [P, T], F32)
+        nc.vector.memset(gf[:], 0.0)
+        key_s = load_scales("key_s", keys_scales, nc.scalar)
+        temper_t = load_vec("temper_t", temper, nc.sync)
+        key_w = load_words("key_w", keys_words)
+        q_raw = load_rows("q_raw", query, slice(0, Q))
+        th_t = load_vec("th_t", th, nc.sync)
+        hsc_t = load_vec("hsc_t", hsc, nc.sync)
+        g_raw = load_rows("g_raw", gout, slice(0, Q))
+        res_t = load_vec("res_t", reserve, nc.sync)
+        old_t = tile("old_t", [P, T], F32)
+        nc.sync.dma_start(old_t[:], old)
+
+        ident = tile("ident", [P, P], F32)
+        make_identity(nc, ident[:])
+
+        def scaled(name, vec, factor):
+            res = tile(name, list(vec.shape), F32)
+            nc.gpsimd.tensor_scalar(res[:], vec[:], factor, 0.0, ALU.mult, ALU.add)
+            return res
+
+        def gather(name, win, dtype, first, count):
+            got = tile(name, [P, count], dtype)
+            nc.vector.tensor_copy(got[:], win[:].indirect(offsets[:, first // 16:(first + count) // 16]))
+            return got
+
+        tab_gs = [gather("tab_gs%d" % h, tab_s, U8, h * CH, CH) for h in range(CHUNKS)]
+
+        w_codes = tile("w_codes", [P, R], U32)
+        w_scales = tile("w_scales", [P, R], U8)
+        MH = HALF // PACK
+        for h in range(2):
+            w_bf = tile("w_bf%d" % h, [P, PACK, MH, PACK], BF16)
+            dst = w_bf[:].rearrange("p t m j -> p m j t")
+            src = w_raw[h][:].rearrange("p j (m t) -> p m j t", t=PACK)
+            nc.scalar.activation(dst, src, ACT.Copy)
+            if h == 0:
+                key_gs = gather("key_gs", key_s, U8, 0, I)
+            else:
+                tab_gw = [gather("tab_gw0", tab_w, U16, 0, CH)]
+            for t in range(PACK):
+                cols = slice(t * P + h * MH, t * P + (h + 1) * MH)
+                nc.vector.quantize_mx(out=w_codes[:, cols].bitcast(FP8X4), scales=w_scales[:, cols],
+                                      in_=w_bf[:, t].rearrange("p m j -> p (m j)"))
+
+        tab_gw.append(gather("tab_gw1", tab_w, U16, CH, CH))
+
+        def cast_rows(name, raw, on_scalar):
+            bf = tile(name, [P, Q, PACK], BF16)
+            dst = bf[:].rearrange("p (c i) j -> p c j i", i=LINE)
+            src = raw[:].rearrange("p j (c i) -> p c j i", i=LINE)
+            if on_scalar:
+                nc.scalar.activation(dst, src, ACT.Copy)
+            else:
+                nc.vector.tensor_copy(dst, src)
+            return bf
+
+        def quantize(name, bf):
+            cols = bf.shape[1]
+            codes = tile(name + "_codes", [P, cols], U32)
+            scales = tile(name + "_scales", [P, cols], U8)
+            nc.vector.quantize_mx(out=codes[:].bitcast(FP8X4), scales=scales[:], in_=bf[:].rearrange("p c j -> p (c j)"))
+            return codes, scales
+
+        CB = CH // GROUP // LINE
+        ht = []
+        for h in range(CHUNKS):
+            ht_h = tile("ht%d" % h, [P, GROUP, CB, PACK, LINE], F32)
+            for t in range(PACK):
+                zh = bank("zh%d_%d" % (h, t), "z%d" % t, CH)
+                cols = slice(t * P, (t + 1) * P)
+                nc.tensor.matmul_mx(out=zh[:], lhsT=w_codes[:, cols].bitcast(FP8X4), lhsT_scale=w_scales[:, cols],
+                                    rhs=tab_gw[h][:].bitcast(FP4X4), rhs_scale=tab_gs[h][:], start=True, stop=True)
+                nc.scalar.activation(ht_h[:, :, :, t, :], zh[:].rearrange("p (c i j) -> p j c i", i=LINE, j=GROUP),
+                                     ACT.Exp, scale=temper_t[:, t:t + 1])
+            ht.append(ht_h)
+
+        key_gw = gather("key_gw", key_w, U16, 0, I)
+        q_bf = cast_rows("q_bf", q_raw, False)
+        q_codes, q_scales = quantize("q", q_bf)
+
+        hsc4 = scaled("hsc4", hsc_t, 4.0)
+        nth = scaled("nth", th_t, -1.0)
+        nth2 = scaled("nth2", th_t, -0.5)
+        nres = scaled("nres", res_t, -1.0)
+        inv = []
+        for h in range(CHUNKS):
+            mz_t = bank("mz_t%d" % h, "s%d" % h, P)
+            for j in range(GROUP):
+                nc.tensor.matmul(mz_t[:], ht[h][:, j].rearrange("p c t i -> p (c t i)"), ident[:], is_transpose=True,
+                                 start=(j == 0), stop=(j == GROUP - 1))
+            inv_t = tile("inv_t%d" % h, [P, P], F32)
+            nc.vector.reciprocal(inv_t[:], mz_t[:])
+            inv.append(inv_t)
+            if h == 0:
+                a = bank("a", "a", I)
+                nc.tensor.matmul_mx(out=a[:], lhsT=q_codes[:].bitcast(FP8X4), lhsT_scale=q_scales[:],
+                                    rhs=key_gw[:].bitcast(FP4X4), rhs_scale=key_gs[:], start=True, stop=True)
+                ex = tile("ex", [P, I], F32)
+                nc.scalar.activation(ex[:], a[:], ACT.Exp, bias=nth[:])
+                tanh = tile("tanh", [P, I], F32)
+                nc.scalar.activation(tanh[:], a[:], ACT.Tanh, bias=nth2[:], scale=0.5)
+
+
+        fac = []
+        for h in range(CHUNKS):
+            back = bank("back%d" % h, "b" if h == 0 else "s0", P)
+            nc.tensor.transpose(back[:], inv[h][:], ident[:])
+            fac_h = tile("fac%d" % h, [P, CB, PACK, LINE], F32)
+            back_v = back[:].rearrange("p (c t i) -> p c t i", t=PACK, i=LINE)
+            for t in range(PACK):
+                nc.scalar.activation(fac_h[:, :, t, :], back_v[:, :, t, :], ACT.Copy, scale=hsc4[:, t:t + 1])
+            fac.append(fac_h)
+
+        g_bf = cast_rows("g_bf", g_raw, True)
+        g_codes, g_scales = quantize("g", g_bf)
+
+        p_t = tile("p_t", [P, I], F32)
+        p_sum = tile("p_sum", [P, 1], F32)
+        nc.scalar.activation(p_t[:], ex[:], ACT.Ln, bias=1.0, accum_out=p_sum[:])
+        nz = tile("nz", [P, 1], F32)
+        nc.scalar.activation(nz[:], p_sum[:], ACT.Identity, bias=nres[:], scale=-1.0)
+
+        hs = []
+        for h in range(CHUNKS):
+            hs_h = tile("hs%d" % h, [P, CH, PACK], BF16)
+            nc.vector.tensor_tensor(hs_h[:].rearrange("p (j c i) t -> p j c t i", j=GROUP, i=LINE), ht[h][:],
+                                    fac[h][:].unsqueeze(1).to_broadcast([P, GROUP, CB, PACK, LINE]), ALU.mult)
+            hs.append(hs_h)
+
+        nrz = tile("nrz", [P, 1], F32)
+        nc.vector.reciprocal(nrz[:], nz[:])
+        rz = tile("rz", [P, 1], F32)
+        nc.scalar.activation(rz[:], nrz[:], ACT.Copy, scale=-256.0)
+        sg = tile("sg", [P, I], F32)
+        nc.scalar.activation(sg[:], tanh[:], ACT.Identity, bias=rz[:], scale=rz[:])
+
+        c0 = []
+        for h in range(CHUNKS):
+            h_codes, h_scales = quantize("h%d" % h, hs[h])
+            c0_h = bank("c0_%d" % h, "z%d" % h, CH)
+            nc.tensor.matmul_mx(out=c0_h[:], lhsT=g_codes[:].bitcast(FP8X4), lhsT_scale=g_scales[:],
+                                rhs=h_codes[:].bitcast(FP8X4), rhs_scale=h_scales[:], start=True, stop=True)
+            c0.append(c0_h[:].rearrange("p (j g) -> p g j", j=GROUP))
+
+        def slots(t, h):
+            return t[:, h * CH:(h + 1) * CH].rearrange("p (g j) -> p g j", j=GROUP)
+
+        prod = tile("prod", [P, I], F32)
+        part = [tile("part%d" % h, [P, 1], F32) for h in range(CHUNKS)]
+        for h in range(CHUNKS):
+            nc.vector.scalar_tensor_tensor(slots(prod, h), c0[h], nrz[:], slots(p_t, h), ALU.mult, ALU.mult,
+                                           accum_out=part[h][:])
+        u = tile("u", [P, I], F32)
+        u_first = tile("u_first", [P, CH], F32)
+        nc.scalar.activation(slots(u_first, 0), c0[0], ACT.Identity, bias=part[0][:])
+        nc.scalar.activation(u[:, 0:CH], u_first[:], ACT.Identity, bias=part[1][:])
+        nc.vector.tensor_scalar(slots(u, 1), c0[1], part[0][:], part[1][:], ALU.add, ALU.add)
+        nc.vector.tensor_tensor(gf[:].indirect(offsets[:]), u[:], sg[:], ALU.mult)
+
+        first = 0
+        for n, width in enumerate(STORE):
+            cols = slice(first, first + width)
+            res = tile("res%d" % n, [P, width], F32)
+            nc.vector.tensor_tensor(res[:], old_t[:, cols], gf[:, cols], ALU.add)
+            nc.sync.dma_start(out[:, cols], res[:])
+            first = first + width

@@ -23,7 +23,7 @@ GROUP = I // G
 CHUNKS = 2
 CH = I // CHUNKS
 LINE = 4
-HALF = R // 2
+W_PIECES = (slice(0, 256), slice(256, 384), slice(384, 512))
 STORE = (256, 512, 512, 512, 256)
 
 
@@ -34,8 +34,12 @@ def tile_attend_blrshared_capped_kernel(tc, query, keys_words, keys_scales, th, 
         sb = ctx.enter_context(tc.tile_pool(name="sb", bufs=1))
         ps = ctx.enter_context(tc.psum_pool(name="ps", bufs=1))
 
-        def tile(name, shape, dtype):
-            return sb.tile(shape, dtype, name=name, align_bytes=64)
+        shared = ctx.enter_context(tc.tile_pool(name="shared", bufs=1))
+
+        def tile(name, shape, dtype, tag="", offset=None):
+            if offset is not None:
+                return shared.tile(shape, dtype, name=name, align_bytes=64, offset=offset)
+            return sb.tile(shape, dtype, name=name, align_bytes=64, tag=tag)
 
         def bank(name, tag, cols):
             return ps.tile([P, cols], F32, name=name, tag=tag)
@@ -45,14 +49,14 @@ def tile_attend_blrshared_capped_kernel(tc, query, keys_words, keys_scales, th, 
 
         def load_scales(name, src, queue):
             win = tile(name, [P, T], U8)
-            nc.vector.memset(win[:].bitcast(I32), 0)
+            nc.gpsimd.memset(win[:].bitcast(I32), 0)
             rows = src[0].bitcast(I32).rearrange("(a r) c -> r a c", r=4)
             for r in range(4):
                 queue.dma_start(win[r:P:32, :].bitcast(I32), rows[r])
             return win
 
-        def load_words(name, src):
-            win = tile(name, [P, T], U16)
+        def load_words(name, src, offset=None):
+            win = tile(name, [P, T], U16, offset=offset)
             nc.sync.dma_start(win[:].bitcast(I32), src[0].bitcast(I32))
             return win
 
@@ -67,16 +71,16 @@ def tile_attend_blrshared_capped_kernel(tc, query, keys_words, keys_scales, th, 
             queue.dma_start(vec[:], src.rearrange("(p t) o -> p (t o)", t=n))
             return vec
 
-        w_raw = [load_rows("w_raw0", w1, slice(0, HALF))]
+        w_raw = [load_rows("w_raw0", w1, W_PIECES[0])]
         tab_s = load_scales("tab_s", tab_scales, nc.sync)
-        w_raw.append(load_rows("w_raw1", w1, slice(HALF, R)))
         tab_w = load_words("tab_w", tab_words)
+        w_raw.extend(load_rows("w_raw%d" % n, w1, W_PIECES[n]) for n in (1, 2))
+        temper_t = load_vec("temper_t", temper, nc.sync)
+        q_raw = load_rows("q_raw", query, slice(0, Q))
+        key_s = load_scales("key_s", keys_scales, nc.sync)
+        key_w = load_words("key_w", keys_words, 0)
         gf = tile("gf", [P, T], F32)
         nc.vector.memset(gf[:], 0.0)
-        key_s = load_scales("key_s", keys_scales, nc.scalar)
-        temper_t = load_vec("temper_t", temper, nc.sync)
-        key_w = load_words("key_w", keys_words)
-        q_raw = load_rows("q_raw", query, slice(0, Q))
         th_t = load_vec("th_t", th, nc.sync)
         hsc_t = load_vec("hsc_t", hsc, nc.sync)
         g_raw = load_rows("g_raw", gout, slice(0, Q))
@@ -88,8 +92,8 @@ def tile_attend_blrshared_capped_kernel(tc, query, keys_words, keys_scales, th, 
         make_identity(nc, ident[:])
 
         def scaled(name, vec, factor):
-            res = tile(name, list(vec.shape), F32)
-            nc.gpsimd.tensor_scalar(res[:], vec[:], factor, 0.0, ALU.mult, ALU.add)
+            res = tile(name, list(vec.shape), F32, name)
+            nc.scalar.activation(res[:], vec[:], ACT.Copy, scale=factor)
             return res
 
         def gather(name, win, dtype, first, count):
@@ -97,35 +101,25 @@ def tile_attend_blrshared_capped_kernel(tc, query, keys_words, keys_scales, th, 
             nc.vector.tensor_copy(got[:], win[:].indirect(offsets[:, first // 16:(first + count) // 16]))
             return got
 
-        tab_gs = [gather("tab_gs%d" % h, tab_s, U8, h * CH, CH) for h in range(CHUNKS)]
+        tab_gs = gather("tab_gs", tab_s, U8, 0, I)
+        tab_gw = gather("tab_gw", tab_w, U16, 0, I)
 
         w_codes = tile("w_codes", [P, R], U32)
         w_scales = tile("w_scales", [P, R], U8)
-        MH = HALF // PACK
-        for h in range(2):
-            w_bf = tile("w_bf%d" % h, [P, PACK, MH, PACK], BF16)
-            dst = w_bf[:].rearrange("p t m j -> p m j t")
-            src = w_raw[h][:].rearrange("p j (m t) -> p m j t", t=PACK)
-            nc.scalar.activation(dst, src, ACT.Copy)
-            if h == 0:
-                key_gs = gather("key_gs", key_s, U8, 0, I)
-            else:
-                tab_gw = [gather("tab_gw0", tab_w, U16, 0, CH)]
-            for t in range(PACK):
-                cols = slice(t * P + h * MH, t * P + (h + 1) * MH)
-                nc.vector.quantize_mx(out=w_codes[:, cols].bitcast(FP8X4), scales=w_scales[:, cols],
-                                      in_=w_bf[:, t].rearrange("p m j -> p (m j)"))
+        w_bf = tile("w_bf", [P, PACK, P, PACK], BF16)
+        for raw, piece in zip(w_raw, W_PIECES):
+            dst = w_bf[:, :, piece.start // PACK:piece.stop // PACK, :].rearrange("p t m j -> p m j t")
+            nc.scalar.activation(dst, raw[:].rearrange("p j (m t) -> p m j t", t=PACK), ACT.Copy)
+        for t in range(PACK):
+            cols = slice(t * P, (t + 1) * P)
+            nc.vector.quantize_mx(out=w_codes[:, cols].bitcast(FP8X4), scales=w_scales[:, cols],
+                                  in_=w_bf[:, t].rearrange("p m j -> p (m j)"))
 
-        tab_gw.append(gather("tab_gw1", tab_w, U16, CH, CH))
-
-        def cast_rows(name, raw, on_scalar):
-            bf = tile(name, [P, Q, PACK], BF16)
+        def cast_rows(name, raw, offset=None):
+            bf = tile(name, [P, Q, PACK], BF16, offset=offset)
             dst = bf[:].rearrange("p (c i) j -> p c j i", i=LINE)
             src = raw[:].rearrange("p j (c i) -> p c j i", i=LINE)
-            if on_scalar:
-                nc.scalar.activation(dst, src, ACT.Copy)
-            else:
-                nc.vector.tensor_copy(dst, src)
+            nc.scalar.activation(dst, src, ACT.Copy)
             return bf
 
         def quantize(name, bf):
@@ -135,6 +129,11 @@ def tile_attend_blrshared_capped_kernel(tc, query, keys_words, keys_scales, th, 
             nc.vector.quantize_mx(out=codes[:].bitcast(FP8X4), scales=scales[:], in_=bf[:].rearrange("p c j -> p (c j)"))
             return codes, scales
 
+        q_bf = cast_rows("q_bf", q_raw)
+        q_codes, q_scales = quantize("q", q_bf)
+        key_gs = gather("key_gs", key_s, U8, 0, I)
+        key_gw = gather("key_gw", key_w, U16, 0, I)
+
         CB = CH // GROUP // LINE
         ht = []
         for h in range(CHUNKS):
@@ -143,15 +142,14 @@ def tile_attend_blrshared_capped_kernel(tc, query, keys_words, keys_scales, th, 
                 zh = bank("zh%d_%d" % (h, t), "z%d" % t, CH)
                 cols = slice(t * P, (t + 1) * P)
                 nc.tensor.matmul_mx(out=zh[:], lhsT=w_codes[:, cols].bitcast(FP8X4), lhsT_scale=w_scales[:, cols],
-                                    rhs=tab_gw[h][:].bitcast(FP4X4), rhs_scale=tab_gs[h][:], start=True, stop=True)
+                                    rhs=tab_gw[:, h * CH:(h + 1) * CH].bitcast(FP4X4), rhs_scale=tab_gs[:, h * CH:(h + 1) * CH], start=True, stop=True)
                 nc.scalar.activation(ht_h[:, :, :, t, :], zh[:].rearrange("p (c i j) -> p j c i", i=LINE, j=GROUP),
                                      ACT.Exp, scale=temper_t[:, t:t + 1])
             ht.append(ht_h)
 
-        key_gw = gather("key_gw", key_w, U16, 0, I)
-        q_bf = cast_rows("q_bf", q_raw, False)
-        q_codes, q_scales = quantize("q", q_bf)
 
+        ident_late = tile("ident_late", [P, P], F32, offset=2048)
+        nc.scalar.copy(ident_late[:], ident[:])
         hsc4 = scaled("hsc4", hsc_t, 4.0)
         nth = scaled("nth", th_t, -1.0)
         nth2 = scaled("nth2", th_t, -0.5)
@@ -160,9 +158,9 @@ def tile_attend_blrshared_capped_kernel(tc, query, keys_words, keys_scales, th, 
         for h in range(CHUNKS):
             mz_t = bank("mz_t%d" % h, "s%d" % h, P)
             for j in range(GROUP):
-                nc.tensor.matmul(mz_t[:], ht[h][:, j].rearrange("p c t i -> p (c t i)"), ident[:], is_transpose=True,
+                nc.tensor.matmul(mz_t[:], ht[h][:, j].rearrange("p c t i -> p (c t i)"), (ident, ident_late)[h][:], is_transpose=True,
                                  start=(j == 0), stop=(j == GROUP - 1))
-            inv_t = tile("inv_t%d" % h, [P, P], F32)
+            inv_t = tile("inv_t%d" % h, [P, P], F32, offset=1024 * h)
             nc.vector.reciprocal(inv_t[:], mz_t[:])
             inv.append(inv_t)
             if h == 0:
@@ -174,7 +172,6 @@ def tile_attend_blrshared_capped_kernel(tc, query, keys_words, keys_scales, th, 
                 tanh = tile("tanh", [P, I], F32)
                 nc.scalar.activation(tanh[:], a[:], ACT.Tanh, bias=nth2[:], scale=0.5)
 
-
         fac = []
         for h in range(CHUNKS):
             back = bank("back%d" % h, "b" if h == 0 else "s0", P)
@@ -184,12 +181,12 @@ def tile_attend_blrshared_capped_kernel(tc, query, keys_words, keys_scales, th, 
             for t in range(PACK):
                 nc.scalar.activation(fac_h[:, :, t, :], back_v[:, :, t, :], ACT.Copy, scale=hsc4[:, t:t + 1])
             fac.append(fac_h)
+            if h == 0:
+                g_bf = cast_rows("g_bf", g_raw, 0)
 
-        g_bf = cast_rows("g_bf", g_raw, True)
-        g_codes, g_scales = quantize("g", g_bf)
 
         p_t = tile("p_t", [P, I], F32)
-        p_sum = tile("p_sum", [P, 1], F32)
+        p_sum = tile("p_sum", [P, 1], F32, "hsc4")
         nc.scalar.activation(p_t[:], ex[:], ACT.Ln, bias=1.0, accum_out=p_sum[:])
         nz = tile("nz", [P, 1], F32)
         nc.scalar.activation(nz[:], p_sum[:], ACT.Identity, bias=nres[:], scale=-1.0)
@@ -200,6 +197,8 @@ def tile_attend_blrshared_capped_kernel(tc, query, keys_words, keys_scales, th, 
             nc.vector.tensor_tensor(hs_h[:].rearrange("p (j c i) t -> p j c t i", j=GROUP, i=LINE), ht[h][:],
                                     fac[h][:].unsqueeze(1).to_broadcast([P, GROUP, CB, PACK, LINE]), ALU.mult)
             hs.append(hs_h)
+            if h == 0:
+                g_codes, g_scales = quantize("g", g_bf)
 
         nrz = tile("nrz", [P, 1], F32)
         nc.vector.reciprocal(nrz[:], nz[:])

@@ -49,7 +49,7 @@ def tile_attend_blrshared_capped_kernel(tc, query, keys_words, keys_scales, th, 
 
         def load_scales(name, src, queue):
             win = tile(name, [P, T], U8)
-            nc.gpsimd.memset(win[:].bitcast(I32), 0)
+            nc.vector.memset(win[:].bitcast(I32), 0)
             rows = src[0].bitcast(I32).rearrange("(a r) c -> r a c", r=4)
             for r in range(4):
                 queue.dma_start(win[r:P:32, :].bitcast(I32), rows[r])
@@ -71,12 +71,11 @@ def tile_attend_blrshared_capped_kernel(tc, query, keys_words, keys_scales, th, 
             queue.dma_start(vec[:], src.rearrange("(p t) o -> p (t o)", t=n))
             return vec
 
-        w_raw = [load_rows("w_raw0", w1, W_PIECES[0])]
+        q_raw = load_rows("q_raw", query, slice(0, Q))
         tab_s = load_scales("tab_s", tab_scales, nc.sync)
         tab_w = load_words("tab_w", tab_words)
-        w_raw.extend(load_rows("w_raw%d" % n, w1, W_PIECES[n]) for n in (1, 2))
+        w_raw = load_rows("w_raw", w1, slice(0, R))
         temper_t = load_vec("temper_t", temper, nc.sync)
-        q_raw = load_rows("q_raw", query, slice(0, Q))
         key_s = load_scales("key_s", keys_scales, nc.sync)
         key_w = load_words("key_w", keys_words, 0)
         gf = tile("gf", [P, T], F32)
@@ -101,20 +100,6 @@ def tile_attend_blrshared_capped_kernel(tc, query, keys_words, keys_scales, th, 
             nc.vector.tensor_copy(got[:], win[:].indirect(offsets[:, first // 16:(first + count) // 16]))
             return got
 
-        tab_gs = gather("tab_gs", tab_s, U8, 0, I)
-        tab_gw = gather("tab_gw", tab_w, U16, 0, I)
-
-        w_codes = tile("w_codes", [P, R], U32)
-        w_scales = tile("w_scales", [P, R], U8)
-        w_bf = tile("w_bf", [P, PACK, P, PACK], BF16)
-        for raw, piece in zip(w_raw, W_PIECES):
-            dst = w_bf[:, :, piece.start // PACK:piece.stop // PACK, :].rearrange("p t m j -> p m j t")
-            nc.scalar.activation(dst, raw[:].rearrange("p j (m t) -> p m j t", t=PACK), ACT.Copy)
-        for t in range(PACK):
-            cols = slice(t * P, (t + 1) * P)
-            nc.vector.quantize_mx(out=w_codes[:, cols].bitcast(FP8X4), scales=w_scales[:, cols],
-                                  in_=w_bf[:, t].rearrange("p m j -> p (m j)"))
-
         def cast_rows(name, raw, offset=None):
             bf = tile(name, [P, Q, PACK], BF16, offset=offset)
             dst = bf[:].rearrange("p (c i) j -> p c j i", i=LINE)
@@ -131,6 +116,24 @@ def tile_attend_blrshared_capped_kernel(tc, query, keys_words, keys_scales, th, 
 
         q_bf = cast_rows("q_bf", q_raw)
         q_codes, q_scales = quantize("q", q_bf)
+        tab_gs = gather("tab_gs", tab_s, U8, 0, I)
+        tab_gw = gather("tab_gw", tab_w, U16, 0, I)
+
+        w_codes = tile("w_codes", [P, R], U32)
+        w_scales = tile("w_scales", [P, R], U8)
+        w_src = w_raw[:].rearrange("p j (m u t) -> p u m j t", u=2, t=2)
+        for u in range(2):
+            w_bf = tile("w_bf%d" % u, [P, 2, P, PACK], BF16)
+            dst = w_bf[:].rearrange("p t m j -> p m j t")
+            if u == 0:
+                nc.vector.tensor_copy(dst, w_src[:, u])
+            else:
+                nc.scalar.activation(dst, w_src[:, u], ACT.Copy)
+            for t in range(2):
+                cols = slice((2 * u + t) * P, (2 * u + t + 1) * P)
+                nc.vector.quantize_mx(out=w_codes[:, cols].bitcast(FP8X4), scales=w_scales[:, cols],
+                                      in_=w_bf[:, t].rearrange("p m j -> p (m j)"))
+
         key_gs = gather("key_gs", key_s, U8, 0, I)
         key_gw = gather("key_gw", key_w, U16, 0, I)
 
@@ -160,7 +163,7 @@ def tile_attend_blrshared_capped_kernel(tc, query, keys_words, keys_scales, th, 
             for j in range(GROUP):
                 nc.tensor.matmul(mz_t[:], ht[h][:, j].rearrange("p c t i -> p (c t i)"), (ident, ident_late)[h][:], is_transpose=True,
                                  start=(j == 0), stop=(j == GROUP - 1))
-            inv_t = tile("inv_t%d" % h, [P, P], F32, offset=1024 * h)
+            inv_t = tile("inv_t%d" % h, [P, P], F32, offset=768 * (h + 1))
             nc.vector.reciprocal(inv_t[:], mz_t[:])
             inv.append(inv_t)
             if h == 0:
@@ -172,48 +175,49 @@ def tile_attend_blrshared_capped_kernel(tc, query, keys_words, keys_scales, th, 
                 tanh = tile("tanh", [P, I], F32)
                 nc.scalar.activation(tanh[:], a[:], ACT.Tanh, bias=nth2[:], scale=0.5)
 
-        fac = []
-        for h in range(CHUNKS):
-            back = bank("back%d" % h, "b" if h == 0 else "s0", P)
+        def turn_back(h, tag):
+            back = bank("back%d" % h, tag, P)
             nc.tensor.transpose(back[:], inv[h][:], ident[:])
-            fac_h = tile("fac%d" % h, [P, CB, PACK, LINE], F32)
-            back_v = back[:].rearrange("p (c t i) -> p c t i", t=PACK, i=LINE)
-            for t in range(PACK):
-                nc.scalar.activation(fac_h[:, :, t, :], back_v[:, :, t, :], ACT.Copy, scale=hsc4[:, t:t + 1])
-            fac.append(fac_h)
-            if h == 0:
-                g_bf = cast_rows("g_bf", g_raw, 0)
+            return back[:].rearrange("p (c t i) -> p c t i", t=PACK, i=LINE)
 
+        def weigh(h, fac):
+            hs = tile("hs%d" % h, [P, CH, PACK], BF16)
+            nc.vector.tensor_tensor(hs[:].rearrange("p (j c i) t -> p j c t i", j=GROUP, i=LINE), ht[h][:],
+                                    fac[:].unsqueeze(1).to_broadcast([P, GROUP, CB, PACK, LINE]), ALU.mult)
+            return hs
 
+        def read(h, h_codes, h_scales):
+            c0_h = bank("c0_%d" % h, "z%d" % h, CH)
+            nc.tensor.matmul_mx(out=c0_h[:], lhsT=g_codes[:].bitcast(FP8X4), lhsT_scale=g_scales[:],
+                                rhs=h_codes[:].bitcast(FP8X4), rhs_scale=h_scales[:], start=True, stop=True)
+            return c0_h[:].rearrange("p (j g) -> p g j", j=GROUP)
+
+        back0 = turn_back(0, "b")
+        fac0 = tile("fac0", [P, CB, PACK, LINE], F32)
+        for t in range(PACK):
+            nc.scalar.activation(fac0[:, :, t, :], back0[:, :, t, :], ACT.Copy, scale=hsc4[:, t:t + 1])
+        g_bf = cast_rows("g_bf", g_raw, 0)
         p_t = tile("p_t", [P, I], F32)
-        p_sum = tile("p_sum", [P, 1], F32, "hsc4")
+        p_sum = tile("p_sum", [P, 1], F32, offset=1088)
         nc.scalar.activation(p_t[:], ex[:], ACT.Ln, bias=1.0, accum_out=p_sum[:])
         nz = tile("nz", [P, 1], F32)
         nc.scalar.activation(nz[:], p_sum[:], ACT.Identity, bias=nres[:], scale=-1.0)
 
-        hs = []
-        for h in range(CHUNKS):
-            hs_h = tile("hs%d" % h, [P, CH, PACK], BF16)
-            nc.vector.tensor_tensor(hs_h[:].rearrange("p (j c i) t -> p j c t i", j=GROUP, i=LINE), ht[h][:],
-                                    fac[h][:].unsqueeze(1).to_broadcast([P, GROUP, CB, PACK, LINE]), ALU.mult)
-            hs.append(hs_h)
-            if h == 0:
-                g_codes, g_scales = quantize("g", g_bf)
-
+        back1 = turn_back(1, "s0")
+        hs0 = weigh(0, fac0)
+        fac1 = tile("fac1", [P, CB, PACK, LINE], F32)
+        nc.vector.tensor_tensor(fac1[:], back1, hsc4[:].unsqueeze(1).unsqueeze(3).to_broadcast([P, CB, PACK, LINE]), ALU.mult)
+        h0 = quantize("h0", hs0)
+        g_codes, g_scales = quantize("g", g_bf)
+        hs1 = weigh(1, fac1)
         nrz = tile("nrz", [P, 1], F32)
         nc.vector.reciprocal(nrz[:], nz[:])
+        h1 = quantize("h1", hs1)
         rz = tile("rz", [P, 1], F32)
         nc.scalar.activation(rz[:], nrz[:], ACT.Copy, scale=-256.0)
         sg = tile("sg", [P, I], F32)
         nc.scalar.activation(sg[:], tanh[:], ACT.Identity, bias=rz[:], scale=rz[:])
-
-        c0 = []
-        for h in range(CHUNKS):
-            h_codes, h_scales = quantize("h%d" % h, hs[h])
-            c0_h = bank("c0_%d" % h, "z%d" % h, CH)
-            nc.tensor.matmul_mx(out=c0_h[:], lhsT=g_codes[:].bitcast(FP8X4), lhsT_scale=g_scales[:],
-                                rhs=h_codes[:].bitcast(FP8X4), rhs_scale=h_scales[:], start=True, stop=True)
-            c0.append(c0_h[:].rearrange("p (j g) -> p g j", j=GROUP))
+        c0 = [read(0, *h0), read(1, *h1)]
 
         def slots(t, h):
             return t[:, h * CH:(h + 1) * CH].rearrange("p (g j) -> p g j", j=GROUP)

@@ -19,225 +19,238 @@ ACT = mybir.ActivationFunctionType
 
 P = 128
 PACK = 4
+QUADRANT = 32
 GROUP = I // G
-CHUNKS = 2
-CH = I // CHUNKS
-LINE = 4
-W_PIECES = (slice(0, 256), slice(256, 384), slice(384, 512))
-STORE = (256, 512, 512, 512, 256)
+HALF = I // 2
+RUN = 4
+RUNS = HALF // GROUP // RUN
+PIECES = (256, 512, 512, 512, 256)
+
+KEY_WORDS_AT = 0
+INV_AT = (768, 1536)
+IDENT_LATE_AT = 2048
+GOUT_BF_AT = 0
+P_SUM_AT = 1088
 
 
 def tile_attend_blrshared_capped_kernel(tc, query, keys_words, keys_scales, th, reserve, tab_words, tab_scales,
                                          w1, temper, gout, hsc, old, offs, out):
     nc = tc.nc
     with ExitStack() as ctx:
-        sb = ctx.enter_context(tc.tile_pool(name="sb", bufs=1))
-        ps = ctx.enter_context(tc.psum_pool(name="ps", bufs=1))
+        keep = ctx.enter_context(tc.tile_pool(name="keep", bufs=1))
+        psum = ctx.enter_context(tc.psum_pool(name="psum", bufs=1))
+        reuse = ctx.enter_context(tc.tile_pool(name="reuse", bufs=1))
 
-        shared = ctx.enter_context(tc.tile_pool(name="shared", bufs=1))
-
-        def tile(name, shape, dtype, tag="", offset=None):
-            if offset is not None:
-                return shared.tile(shape, dtype, name=name, align_bytes=64, offset=offset)
-            return sb.tile(shape, dtype, name=name, align_bytes=64, tag=tag)
+        def tile(name, shape, dtype, at=None):
+            if at is None:
+                return keep.tile(shape, dtype, name=name, align_bytes=64)
+            return reuse.tile(shape, dtype, name=name, align_bytes=64, offset=at)
 
         def bank(name, tag, cols):
-            return ps.tile([P, cols], F32, name=name, tag=tag)
+            return psum.tile([P, cols], F32, name=name, tag=tag)
 
-        offsets = sb.tile([P, I // 16], U16, name="offsets")
-        nc.sync.dma_start(offsets[:], offs)
+        def half(h):
+            return slice(h * HALF, (h + 1) * HALF)
 
-        def load_scales(name, src, queue):
-            win = tile(name, [P, T], U8)
-            nc.vector.memset(win[:].bitcast(I32), 0)
-            rows = src[0].bitcast(I32).rearrange("(a r) c -> r a c", r=4)
-            for r in range(4):
-                queue.dma_start(win[r:P:32, :].bitcast(I32), rows[r])
-            return win
+        def load_words(name, src, at=None):
+            window = tile(name, [P, T], U16, at)
+            nc.sync.dma_start(window[:].bitcast(I32), src[0].bitcast(I32))
+            return window
 
-        def load_words(name, src, offset=None):
-            win = tile(name, [P, T], U16, offset=offset)
-            nc.sync.dma_start(win[:].bitcast(I32), src[0].bitcast(I32))
-            return win
+        def load_scales(name, src):
+            window = tile(name, [P, T], U8)
+            nc.vector.memset(window[:].bitcast(I32), 0)
+            rows = src[0].bitcast(I32).rearrange("(A s) c -> s A c", s=4)
+            for s in range(4):
+                nc.sync.dma_start(window[s:P:QUADRANT, :].bitcast(I32), rows[s])
+            return window
 
-        def load_rows(name, src, cols):
-            raw = tile(name, [P, PACK, cols.stop - cols.start], F32)
-            nc.sync.dma_start(raw[:], src.rearrange("(p j) c -> p j c", j=PACK)[:, :, cols])
+        def load_rows(name, src):
+            raw = tile(name, [P, PACK, src.shape[1]], F32)
+            nc.sync.dma_start(raw[:], src.rearrange("(p t) c -> p t c", t=PACK))
             return raw
 
-        def load_vec(name, src, queue):
+        def load_vec(name, src):
             n = src.shape[0] // P
             vec = tile(name, [P, n], F32)
-            queue.dma_start(vec[:], src.rearrange("(p t) o -> p (t o)", t=n))
+            nc.sync.dma_start(vec[:], src.rearrange("(p t) o -> p (t o)", t=n))
             return vec
 
-        q_raw = load_rows("q_raw", query, slice(0, Q))
-        tab_s = load_scales("tab_s", tab_scales, nc.sync)
+        offsets = keep.tile([P, I // 16], U16, name="offsets")
+        nc.sync.dma_start(offsets[:], offs)
         tab_w = load_words("tab_w", tab_words)
-        w_raw = load_rows("w_raw", w1, slice(0, R))
-        temper_t = load_vec("temper_t", temper, nc.sync)
-        key_s = load_scales("key_s", keys_scales, nc.sync)
-        key_w = load_words("key_w", keys_words, 0)
+        tab_s = load_scales("tab_s", tab_scales)
+        w_raw = load_rows("w_raw", w1)
+        temper_t = load_vec("temper_t", temper)
+        q_raw = load_rows("q_raw", query)
+        key_s = load_scales("key_s", keys_scales)
+        key_w = load_words("key_w", keys_words, KEY_WORDS_AT)
         gf = tile("gf", [P, T], F32)
         nc.vector.memset(gf[:], 0.0)
-        th_t = load_vec("th_t", th, nc.sync)
-        hsc_t = load_vec("hsc_t", hsc, nc.sync)
-        g_raw = load_rows("g_raw", gout, slice(0, Q))
-        res_t = load_vec("res_t", reserve, nc.sync)
+        th_t = load_vec("th_t", th)
+        hsc_t = load_vec("hsc_t", hsc)
+        g_raw = load_rows("g_raw", gout)
+        reserve_t = load_vec("reserve_t", reserve)
         old_t = tile("old_t", [P, T], F32)
         nc.sync.dma_start(old_t[:], old)
 
         ident = tile("ident", [P, P], F32)
         make_identity(nc, ident[:])
 
-        def scaled(name, vec, factor):
-            res = tile(name, list(vec.shape), F32, name)
-            nc.scalar.activation(res[:], vec[:], ACT.Copy, scale=factor)
-            return res
+        def gather(name, window, dtype):
+            listed = tile(name, [P, I], dtype)
+            nc.vector.tensor_copy(listed[:], window[:].indirect(offsets[:]))
+            return listed
 
-        def gather(name, win, dtype, first, count):
-            got = tile(name, [P, count], dtype)
-            nc.vector.tensor_copy(got[:], win[:].indirect(offsets[:, first // 16:(first + count) // 16]))
-            return got
+        def on_vector(dst, src):
+            nc.vector.tensor_copy(dst, src)
 
-        def cast_rows(name, raw, offset=None):
-            bf = tile(name, [P, Q, PACK], BF16, offset=offset)
-            dst = bf[:].rearrange("p (c i) j -> p c j i", i=LINE)
-            src = raw[:].rearrange("p j (c i) -> p c j i", i=LINE)
+        def on_scalar(dst, src):
             nc.scalar.activation(dst, src, ACT.Copy)
+
+        def interleave(name, raw, cast, at=None):
+            bf = tile(name, [P, Q, PACK], BF16, at)
+            cast(bf[:].rearrange("p (c n) t -> p c t n", n=RUN), raw[:].rearrange("p t (c n) -> p c t n", n=RUN))
             return bf
 
         def quantize(name, bf):
             cols = bf.shape[1]
             codes = tile(name + "_codes", [P, cols], U32)
             scales = tile(name + "_scales", [P, cols], U8)
-            nc.vector.quantize_mx(out=codes[:].bitcast(FP8X4), scales=scales[:], in_=bf[:].rearrange("p c j -> p (c j)"))
+            nc.vector.quantize_mx(out=codes[:].bitcast(FP8X4), scales=scales[:],
+                                  in_=bf[:].rearrange("p c t -> p (c t)"))
             return codes, scales
 
-        q_bf = cast_rows("q_bf", q_raw)
-        q_codes, q_scales = quantize("q", q_bf)
-        tab_gs = gather("tab_gs", tab_s, U8, 0, I)
-        tab_gw = gather("tab_gw", tab_w, U16, 0, I)
+        def times(name, vec, factor):
+            product = tile(name, list(vec.shape), F32)
+            nc.scalar.activation(product[:], vec[:], ACT.Copy, scale=factor)
+            return product
+
+        tab_gw = gather("tab_gw", tab_w, U16)
+        tab_gs = gather("tab_gs", tab_s, U8)
 
         w_codes = tile("w_codes", [P, R], U32)
         w_scales = tile("w_scales", [P, R], U8)
-        w_src = w_raw[:].rearrange("p j (m u t) -> p u m j t", u=2, t=2)
-        for u in range(2):
-            w_bf = tile("w_bf%d" % u, [P, 2, P, PACK], BF16)
-            dst = w_bf[:].rearrange("p t m j -> p m j t")
-            if u == 0:
-                nc.vector.tensor_copy(dst, w_src[:, u])
-            else:
-                nc.scalar.activation(dst, w_src[:, u], ACT.Copy)
-            for t in range(2):
-                cols = slice((2 * u + t) * P, (2 * u + t + 1) * P)
+        w_pairs = w_raw[:].rearrange("p j (m e f) -> p e m j f", e=2, f=2)
+        for e, cast in enumerate((on_vector, on_scalar)):
+            w_bf = tile("w_bf%d" % e, [P, 2, P, PACK], BF16)
+            cast(w_bf[:].rearrange("p f m j -> p m j f"), w_pairs[:, e])
+            for f in range(2):
+                cols = slice((2 * e + f) * P, (2 * e + f + 1) * P)
                 nc.vector.quantize_mx(out=w_codes[:, cols].bitcast(FP8X4), scales=w_scales[:, cols],
-                                      in_=w_bf[:, t].rearrange("p m j -> p (m j)"))
+                                      in_=w_bf[:, f].rearrange("p m j -> p (m j)"))
 
-        key_gs = gather("key_gs", key_s, U8, 0, I)
-        key_gw = gather("key_gw", key_w, U16, 0, I)
+        q_bf = interleave("q_bf", q_raw, on_vector)
+        key_gs = gather("key_gs", key_s, U8)
+        q_codes, q_scales = quantize("q", q_bf)
+        key_gw = gather("key_gw", key_w, U16)
 
-        CB = CH // GROUP // LINE
         ht = []
-        for h in range(CHUNKS):
-            ht_h = tile("ht%d" % h, [P, GROUP, CB, PACK, LINE], F32)
+        for h in range(2):
+            ht_h = tile("ht%d" % h, [P, GROUP, RUNS, PACK, RUN], F32)
             for t in range(PACK):
-                zh = bank("zh%d_%d" % (h, t), "z%d" % t, CH)
+                zh = bank("zh%d_%d" % (h, t), "z%d" % t, HALF)
                 cols = slice(t * P, (t + 1) * P)
                 nc.tensor.matmul_mx(out=zh[:], lhsT=w_codes[:, cols].bitcast(FP8X4), lhsT_scale=w_scales[:, cols],
-                                    rhs=tab_gw[:, h * CH:(h + 1) * CH].bitcast(FP4X4), rhs_scale=tab_gs[:, h * CH:(h + 1) * CH], start=True, stop=True)
-                nc.scalar.activation(ht_h[:, :, :, t, :], zh[:].rearrange("p (c i j) -> p j c i", i=LINE, j=GROUP),
+                                    rhs=tab_gw[:, half(h)].bitcast(FP4X4), rhs_scale=tab_gs[:, half(h)],
+                                    start=True, stop=True)
+                nc.scalar.activation(ht_h[:, :, :, t, :], zh[:].rearrange("p (c n j) -> p j c n", n=RUN, j=GROUP),
                                      ACT.Exp, scale=temper_t[:, t:t + 1])
             ht.append(ht_h)
 
-
-        ident_late = tile("ident_late", [P, P], F32, offset=2048)
+        ident_late = tile("ident_late", [P, P], F32, IDENT_LATE_AT)
         nc.scalar.copy(ident_late[:], ident[:])
-        hsc4 = scaled("hsc4", hsc_t, 4.0)
-        nth = scaled("nth", th_t, -1.0)
-        nth2 = scaled("nth2", th_t, -0.5)
-        nres = scaled("nres", res_t, -1.0)
-        inv = []
-        for h in range(CHUNKS):
-            mz_t = bank("mz_t%d" % h, "s%d" % h, P)
+        hsc4 = times("hsc4", hsc_t, 4.0)
+        neg_th = times("neg_th", th_t, -1.0)
+        neg_half_th = times("neg_half_th", th_t, -0.5)
+        neg_reserve = times("neg_reserve", reserve_t, -1.0)
+
+        def inverse_sums(h, identity):
+            mz_turned = bank("mz_turned%d" % h, "s%d" % h, P)
             for j in range(GROUP):
-                nc.tensor.matmul(mz_t[:], ht[h][:, j].rearrange("p c t i -> p (c t i)"), (ident, ident_late)[h][:], is_transpose=True,
-                                 start=(j == 0), stop=(j == GROUP - 1))
-            inv_t = tile("inv_t%d" % h, [P, P], F32, offset=768 * (h + 1))
-            nc.vector.reciprocal(inv_t[:], mz_t[:])
-            inv.append(inv_t)
-            if h == 0:
-                a = bank("a", "a", I)
-                nc.tensor.matmul_mx(out=a[:], lhsT=q_codes[:].bitcast(FP8X4), lhsT_scale=q_scales[:],
-                                    rhs=key_gw[:].bitcast(FP4X4), rhs_scale=key_gs[:], start=True, stop=True)
-                ex = tile("ex", [P, I], F32)
-                nc.scalar.activation(ex[:], a[:], ACT.Exp, bias=nth[:])
-                tanh = tile("tanh", [P, I], F32)
-                nc.scalar.activation(tanh[:], a[:], ACT.Tanh, bias=nth2[:], scale=0.5)
+                nc.tensor.matmul(mz_turned[:], ht[h][:, j].rearrange("p c t n -> p (c t n)"), identity[:],
+                                 is_transpose=True, start=(j == 0), stop=(j == GROUP - 1))
+            inv_turned = tile("inv_turned%d" % h, [P, P], F32, INV_AT[h])
+            nc.vector.reciprocal(inv_turned[:], mz_turned[:])
+            return inv_turned
 
-        def turn_back(h, tag):
-            back = bank("back%d" % h, tag, P)
-            nc.tensor.transpose(back[:], inv[h][:], ident[:])
-            return back[:].rearrange("p (c t i) -> p c t i", t=PACK, i=LINE)
+        def turn_back(h, inv_turned, tag):
+            inv = bank("inv%d" % h, tag, P)
+            nc.tensor.transpose(inv[:], inv_turned[:], ident[:])
+            return inv[:].rearrange("p (c t n) -> p c t n", t=PACK, n=RUN)
 
-        def weigh(h, fac):
-            hs = tile("hs%d" % h, [P, CH, PACK], BF16)
-            nc.vector.tensor_tensor(hs[:].rearrange("p (j c i) t -> p j c t i", j=GROUP, i=LINE), ht[h][:],
-                                    fac[:].unsqueeze(1).to_broadcast([P, GROUP, CB, PACK, LINE]), ALU.mult)
+        def weigh(h, factor):
+            hs = tile("hs%d" % h, [P, HALF, PACK], BF16)
+            nc.vector.tensor_tensor(hs[:].rearrange("p (j c n) t -> p j c t n", j=GROUP, n=RUN), ht[h][:],
+                                    factor[:].unsqueeze(1).to_broadcast([P, GROUP, RUNS, PACK, RUN]), ALU.mult)
             return hs
 
-        def read(h, h_codes, h_scales):
-            c0_h = bank("c0_%d" % h, "z%d" % h, CH)
-            nc.tensor.matmul_mx(out=c0_h[:], lhsT=g_codes[:].bitcast(FP8X4), lhsT_scale=g_scales[:],
-                                rhs=h_codes[:].bitcast(FP8X4), rhs_scale=h_scales[:], start=True, stop=True)
-            return c0_h[:].rearrange("p (j g) -> p g j", j=GROUP)
+        inv_turned0 = inverse_sums(0, ident)
 
-        back0 = turn_back(0, "b")
-        fac0 = tile("fac0", [P, CB, PACK, LINE], F32)
+        a = bank("a", "a", I)
+        nc.tensor.matmul_mx(out=a[:], lhsT=q_codes[:].bitcast(FP8X4), lhsT_scale=q_scales[:],
+                            rhs=key_gw[:].bitcast(FP4X4), rhs_scale=key_gs[:], start=True, stop=True)
+        exp_a = tile("exp_a", [P, I], F32)
+        nc.scalar.activation(exp_a[:], a[:], ACT.Exp, bias=neg_th[:])
+        tanh_a = tile("tanh_a", [P, I], F32)
+        nc.scalar.activation(tanh_a[:], a[:], ACT.Tanh, bias=neg_half_th[:], scale=0.5)
+
+        inv_turned1 = inverse_sums(1, ident_late)
+
+        inv0 = turn_back(0, inv_turned0, "b")
+        factor0 = tile("factor0", [P, RUNS, PACK, RUN], F32)
         for t in range(PACK):
-            nc.scalar.activation(fac0[:, :, t, :], back0[:, :, t, :], ACT.Copy, scale=hsc4[:, t:t + 1])
-        g_bf = cast_rows("g_bf", g_raw, 0)
+            nc.scalar.activation(factor0[:, :, t, :], inv0[:, :, t, :], ACT.Copy, scale=hsc4[:, t:t + 1])
+        g_bf = interleave("g_bf", g_raw, on_scalar, GOUT_BF_AT)
         p_t = tile("p_t", [P, I], F32)
-        p_sum = tile("p_sum", [P, 1], F32, offset=1088)
-        nc.scalar.activation(p_t[:], ex[:], ACT.Ln, bias=1.0, accum_out=p_sum[:])
-        nz = tile("nz", [P, 1], F32)
-        nc.scalar.activation(nz[:], p_sum[:], ACT.Identity, bias=nres[:], scale=-1.0)
+        p_sum = tile("p_sum", [P, 1], F32, P_SUM_AT)
+        nc.scalar.activation(p_t[:], exp_a[:], ACT.Ln, bias=1.0, accum_out=p_sum[:])
+        neg_z = tile("neg_z", [P, 1], F32)
+        nc.scalar.activation(neg_z[:], p_sum[:], ACT.Identity, bias=neg_reserve[:], scale=-1.0)
 
-        back1 = turn_back(1, "s0")
-        hs0 = weigh(0, fac0)
-        fac1 = tile("fac1", [P, CB, PACK, LINE], F32)
-        nc.vector.tensor_tensor(fac1[:], back1, hsc4[:].unsqueeze(1).unsqueeze(3).to_broadcast([P, CB, PACK, LINE]), ALU.mult)
-        h0 = quantize("h0", hs0)
+        inv1 = turn_back(1, inv_turned1, "s0")
+        hs0 = weigh(0, factor0)
+        factor1 = tile("factor1", [P, RUNS, PACK, RUN], F32)
+        nc.vector.tensor_tensor(factor1[:], inv1,
+                                hsc4[:].unsqueeze(1).unsqueeze(3).to_broadcast([P, RUNS, PACK, RUN]), ALU.mult)
+        hs0_mx = quantize("hs0", hs0)
         g_codes, g_scales = quantize("g", g_bf)
-        hs1 = weigh(1, fac1)
-        nrz = tile("nrz", [P, 1], F32)
-        nc.vector.reciprocal(nrz[:], nz[:])
-        h1 = quantize("h1", hs1)
-        rz = tile("rz", [P, 1], F32)
-        nc.scalar.activation(rz[:], nrz[:], ACT.Copy, scale=-256.0)
-        sg = tile("sg", [P, I], F32)
-        nc.scalar.activation(sg[:], tanh[:], ACT.Identity, bias=rz[:], scale=rz[:])
-        c0 = [read(0, *h0), read(1, *h1)]
+        hs1 = weigh(1, factor1)
+        neg_inv_z = tile("neg_inv_z", [P, 1], F32)
+        nc.vector.reciprocal(neg_inv_z[:], neg_z[:])
+        hs1_mx = quantize("hs1", hs1)
 
-        def slots(t, h):
-            return t[:, h * CH:(h + 1) * CH].rearrange("p (g j) -> p g j", j=GROUP)
+        inv_z256 = times("inv_z256", neg_inv_z, -256.0)
+        gain = tile("gain", [P, I], F32)
+        nc.scalar.activation(gain[:], tanh_a[:], ACT.Identity, bias=inv_z256[:], scale=inv_z256[:])
 
-        prod = tile("prod", [P, I], F32)
-        part = [tile("part%d" % h, [P, 1], F32) for h in range(CHUNKS)]
-        for h in range(CHUNKS):
-            nc.vector.scalar_tensor_tensor(slots(prod, h), c0[h], nrz[:], slots(p_t, h), ALU.mult, ALU.mult,
-                                           accum_out=part[h][:])
-        u = tile("u", [P, I], F32)
-        u_first = tile("u_first", [P, CH], F32)
-        nc.scalar.activation(slots(u_first, 0), c0[0], ACT.Identity, bias=part[0][:])
-        nc.scalar.activation(u[:, 0:CH], u_first[:], ACT.Identity, bias=part[1][:])
-        nc.vector.tensor_scalar(slots(u, 1), c0[1], part[0][:], part[1][:], ALU.add, ALU.add)
-        nc.vector.tensor_tensor(gf[:].indirect(offsets[:]), u[:], sg[:], ALU.mult)
+        c0 = []
+        for h, (hs_codes, hs_scales) in enumerate((hs0_mx, hs1_mx)):
+            c0_h = bank("c0_%d" % h, "z%d" % h, HALF)
+            nc.tensor.matmul_mx(out=c0_h[:], lhsT=g_codes[:].bitcast(FP8X4), lhsT_scale=g_scales[:],
+                                rhs=hs_codes[:].bitcast(FP8X4), rhs_scale=hs_scales[:], start=True, stop=True)
+            c0.append(c0_h[:].rearrange("p (j g) -> p g j", j=GROUP))
+
+        def by_group(values, h):
+            return values[:, half(h)].rearrange("p (g j) -> p g j", j=GROUP)
+
+        terms = tile("terms", [P, I], F32)
+        neg_s = [tile("neg_s%d" % h, [P, 1], F32) for h in range(2)]
+        for h in range(2):
+            nc.vector.scalar_tensor_tensor(by_group(terms, h), c0[h], neg_inv_z[:], by_group(p_t, h),
+                                           ALU.mult, ALU.mult, accum_out=neg_s[h][:])
+
+        centred = tile("centred", [P, I], F32)
+        partly = tile("partly", [P, HALF], F32)
+        nc.scalar.activation(by_group(partly, 0), c0[0], ACT.Identity, bias=neg_s[0][:])
+        nc.scalar.activation(centred[:, half(0)], partly[:], ACT.Identity, bias=neg_s[1][:])
+        nc.vector.tensor_scalar(by_group(centred, 1), c0[1], neg_s[0][:], neg_s[1][:], ALU.add, ALU.add)
+        nc.vector.tensor_tensor(gf[:].indirect(offsets[:]), centred[:], gain[:], ALU.mult)
 
         first = 0
-        for n, width in enumerate(STORE):
+        for n, width in enumerate(PIECES):
             cols = slice(first, first + width)
-            res = tile("res%d" % n, [P, width], F32)
-            nc.vector.tensor_tensor(res[:], old_t[:, cols], gf[:, cols], ALU.add)
-            nc.sync.dma_start(out[:, cols], res[:])
+            piece = tile("piece%d" % n, [P, width], F32)
+            nc.vector.tensor_tensor(piece[:], old_t[:, cols], gf[:, cols], ALU.add)
+            nc.sync.dma_start(out[:, cols], piece[:])
             first = first + width

from contextlib import ExitStack

import concourse.mybir as mybir
from concourse.masks import make_identity

D, K, R, T, I, Q, G = 512, 512, 512, 2048, 512, 128, 64
FLOPS = 2 * (D * Q * I + K * R * I + R * Q * I)

F32 = mybir.dt.float32
BF16 = mybir.dt.bfloat16
I32 = mybir.dt.int32
U32 = mybir.dt.uint32
U16 = mybir.dt.uint16
U8 = mybir.dt.uint8
FP8X4 = mybir.dt.float8_e4m3fn_x4
FP4X4 = mybir.dt.float4_e2m1fn_x4
ALU = mybir.AluOpType
ACT = mybir.ActivationFunctionType

P = 128
PACK = 4
QUADRANT = 32
GROUP = I // G
HALF = I // 2
RUN = 4
RUNS = HALF // GROUP // RUN
PIECES = (256, 512, 512, 512, 256)

KEY_WORDS_AT = 0
INV_AT = (768, 1536)
IDENT_LATE_AT = 2048
GOUT_BF_AT = 0
P_SUM_AT = 1088


def tile_attend_blrshared_capped_kernel(tc, query, keys_words, keys_scales, th, reserve, tab_words, tab_scales,
                                         w1, temper, gout, hsc, old, offs, out):
    nc = tc.nc
    with ExitStack() as ctx:
        keep = ctx.enter_context(tc.tile_pool(name="keep", bufs=1))
        psum = ctx.enter_context(tc.psum_pool(name="psum", bufs=1))
        reuse = ctx.enter_context(tc.tile_pool(name="reuse", bufs=1))

        def tile(name, shape, dtype, at=None):
            if at is None:
                return keep.tile(shape, dtype, name=name, align_bytes=64)
            return reuse.tile(shape, dtype, name=name, align_bytes=64, offset=at)

        def bank(name, tag, cols):
            return psum.tile([P, cols], F32, name=name, tag=tag)

        def half(h):
            return slice(h * HALF, (h + 1) * HALF)

        def load_words(name, src, at=None):
            window = tile(name, [P, T], U16, at)
            nc.sync.dma_start(window[:].bitcast(I32), src[0].bitcast(I32))
            return window

        def load_scales(name, src):
            window = tile(name, [P, T], U8)
            nc.vector.memset(window[:].bitcast(I32), 0)
            rows = src[0].bitcast(I32).rearrange("(A s) c -> s A c", s=4)
            for s in range(4):
                nc.sync.dma_start(window[s:P:QUADRANT, :].bitcast(I32), rows[s])
            return window

        def load_rows(name, src):
            raw = tile(name, [P, PACK, src.shape[1]], F32)
            nc.sync.dma_start(raw[:], src.rearrange("(p t) c -> p t c", t=PACK))
            return raw

        def load_vec(name, src):
            n = src.shape[0] // P
            vec = tile(name, [P, n], F32)
            nc.sync.dma_start(vec[:], src.rearrange("(p t) o -> p (t o)", t=n))
            return vec

        offsets = keep.tile([P, I // 16], U16, name="offsets")
        nc.sync.dma_start(offsets[:], offs)
        tab_w = load_words("tab_w", tab_words)
        tab_s = load_scales("tab_s", tab_scales)
        w_raw = load_rows("w_raw", w1)
        temper_t = load_vec("temper_t", temper)
        q_raw = load_rows("q_raw", query)
        key_s = load_scales("key_s", keys_scales)
        key_w = load_words("key_w", keys_words, KEY_WORDS_AT)
        gf = tile("gf", [P, T], F32)
        nc.vector.memset(gf[:], 0.0)
        th_t = load_vec("th_t", th)
        hsc_t = load_vec("hsc_t", hsc)
        g_raw = load_rows("g_raw", gout)
        reserve_t = load_vec("reserve_t", reserve)
        old_t = tile("old_t", [P, T], F32)
        nc.sync.dma_start(old_t[:], old)

        ident = tile("ident", [P, P], F32)
        make_identity(nc, ident[:])

        def gather(name, window, dtype):
            listed = tile(name, [P, I], dtype)
            nc.vector.tensor_copy(listed[:], window[:].indirect(offsets[:]))
            return listed

        def on_vector(dst, src):
            nc.vector.tensor_copy(dst, src)

        def on_scalar(dst, src):
            nc.scalar.activation(dst, src, ACT.Copy)

        def interleave(name, raw, cast, at=None):
            bf = tile(name, [P, Q, PACK], BF16, at)
            cast(bf[:].rearrange("p (c n) t -> p c t n", n=RUN), raw[:].rearrange("p t (c n) -> p c t n", n=RUN))
            return bf

        def quantize(name, bf):
            cols = bf.shape[1]
            codes = tile(name + "_codes", [P, cols], U32)
            scales = tile(name + "_scales", [P, cols], U8)
            nc.vector.quantize_mx(out=codes[:].bitcast(FP8X4), scales=scales[:],
                                  in_=bf[:].rearrange("p c t -> p (c t)"))
            return codes, scales

        def times(name, vec, factor):
            product = tile(name, list(vec.shape), F32)
            nc.scalar.activation(product[:], vec[:], ACT.Copy, scale=factor)
            return product

        tab_gw = gather("tab_gw", tab_w, U16)
        tab_gs = gather("tab_gs", tab_s, U8)

        w_codes = tile("w_codes", [P, R], U32)
        w_scales = tile("w_scales", [P, R], U8)
        w_pairs = w_raw[:].rearrange("p j (m e f) -> p e m j f", e=2, f=2)
        for e, cast in enumerate((on_vector, on_scalar)):
            w_bf = tile("w_bf%d" % e, [P, 2, P, PACK], BF16)
            cast(w_bf[:].rearrange("p f m j -> p m j f"), w_pairs[:, e])
            for f in range(2):
                cols = slice((2 * e + f) * P, (2 * e + f + 1) * P)
                nc.vector.quantize_mx(out=w_codes[:, cols].bitcast(FP8X4), scales=w_scales[:, cols],
                                      in_=w_bf[:, f].rearrange("p m j -> p (m j)"))

        q_bf = interleave("q_bf", q_raw, on_vector)
        key_gs = gather("key_gs", key_s, U8)
        q_codes, q_scales = quantize("q", q_bf)
        key_gw = gather("key_gw", key_w, U16)

        ht = []
        for h in range(2):
            ht_h = tile("ht%d" % h, [P, GROUP, RUNS, PACK, RUN], F32)
            for t in range(PACK):
                zh = bank("zh%d_%d" % (h, t), "z%d" % t, HALF)
                cols = slice(t * P, (t + 1) * P)
                nc.tensor.matmul_mx(out=zh[:], lhsT=w_codes[:, cols].bitcast(FP8X4), lhsT_scale=w_scales[:, cols],
                                    rhs=tab_gw[:, half(h)].bitcast(FP4X4), rhs_scale=tab_gs[:, half(h)],
                                    start=True, stop=True)
                nc.scalar.activation(ht_h[:, :, :, t, :], zh[:].rearrange("p (c n j) -> p j c n", n=RUN, j=GROUP),
                                     ACT.Exp, scale=temper_t[:, t:t + 1])
            ht.append(ht_h)

        ident_late = tile("ident_late", [P, P], F32, IDENT_LATE_AT)
        nc.scalar.copy(ident_late[:], ident[:])
        hsc4 = times("hsc4", hsc_t, 4.0)
        neg_th = times("neg_th", th_t, -1.0)
        neg_half_th = times("neg_half_th", th_t, -0.5)
        neg_reserve = times("neg_reserve", reserve_t, -1.0)

        def inverse_sums(h, identity):
            mz_turned = bank("mz_turned%d" % h, "s%d" % h, P)
            for j in range(GROUP):
                nc.tensor.matmul(mz_turned[:], ht[h][:, j].rearrange("p c t n -> p (c t n)"), identity[:],
                                 is_transpose=True, start=(j == 0), stop=(j == GROUP - 1))
            inv_turned = tile("inv_turned%d" % h, [P, P], F32, INV_AT[h])
            nc.vector.reciprocal(inv_turned[:], mz_turned[:])
            return inv_turned

        def turn_back(h, inv_turned, tag):
            inv = bank("inv%d" % h, tag, P)
            nc.tensor.transpose(inv[:], inv_turned[:], ident[:])
            return inv[:].rearrange("p (c t n) -> p c t n", t=PACK, n=RUN)

        def weigh(h, factor):
            hs = tile("hs%d" % h, [P, HALF, PACK], BF16)
            nc.vector.tensor_tensor(hs[:].rearrange("p (j c n) t -> p j c t n", j=GROUP, n=RUN), ht[h][:],
                                    factor[:].unsqueeze(1).to_broadcast([P, GROUP, RUNS, PACK, RUN]), ALU.mult)
            return hs

        inv_turned0 = inverse_sums(0, ident)

        a = bank("a", "a", I)
        nc.tensor.matmul_mx(out=a[:], lhsT=q_codes[:].bitcast(FP8X4), lhsT_scale=q_scales[:],
                            rhs=key_gw[:].bitcast(FP4X4), rhs_scale=key_gs[:], start=True, stop=True)
        exp_a = tile("exp_a", [P, I], F32)
        nc.scalar.activation(exp_a[:], a[:], ACT.Exp, bias=neg_th[:])
        tanh_a = tile("tanh_a", [P, I], F32)
        nc.scalar.activation(tanh_a[:], a[:], ACT.Tanh, bias=neg_half_th[:], scale=0.5)

        inv_turned1 = inverse_sums(1, ident_late)

        inv0 = turn_back(0, inv_turned0, "b")
        factor0 = tile("factor0", [P, RUNS, PACK, RUN], F32)
        for t in range(PACK):
            nc.scalar.activation(factor0[:, :, t, :], inv0[:, :, t, :], ACT.Copy, scale=hsc4[:, t:t + 1])
        g_bf = interleave("g_bf", g_raw, on_scalar, GOUT_BF_AT)
        p_t = tile("p_t", [P, I], F32)
        p_sum = tile("p_sum", [P, 1], F32, P_SUM_AT)
        nc.scalar.activation(p_t[:], exp_a[:], ACT.Ln, bias=1.0, accum_out=p_sum[:])
        neg_z = tile("neg_z", [P, 1], F32)
        nc.scalar.activation(neg_z[:], p_sum[:], ACT.Identity, bias=neg_reserve[:], scale=-1.0)

        inv1 = turn_back(1, inv_turned1, "s0")
        hs0 = weigh(0, factor0)
        factor1 = tile("factor1", [P, RUNS, PACK, RUN], F32)
        nc.vector.tensor_tensor(factor1[:], inv1,
                                hsc4[:].unsqueeze(1).unsqueeze(3).to_broadcast([P, RUNS, PACK, RUN]), ALU.mult)
        hs0_mx = quantize("hs0", hs0)
        g_codes, g_scales = quantize("g", g_bf)
        hs1 = weigh(1, factor1)
        neg_inv_z = tile("neg_inv_z", [P, 1], F32)
        nc.vector.reciprocal(neg_inv_z[:], neg_z[:])
        hs1_mx = quantize("hs1", hs1)

        inv_z256 = times("inv_z256", neg_inv_z, -256.0)
        gain = tile("gain", [P, I], F32)
        nc.scalar.activation(gain[:], tanh_a[:], ACT.Identity, bias=inv_z256[:], scale=inv_z256[:])

        c0 = []
        for h, (hs_codes, hs_scales) in enumerate((hs0_mx, hs1_mx)):
            c0_h = bank("c0_%d" % h, "z%d" % h, HALF)
            nc.tensor.matmul_mx(out=c0_h[:], lhsT=g_codes[:].bitcast(FP8X4), lhsT_scale=g_scales[:],
                                rhs=hs_codes[:].bitcast(FP8X4), rhs_scale=hs_scales[:], start=True, stop=True)
            c0.append(c0_h[:].rearrange("p (j g) -> p g j", j=GROUP))

        def by_group(values, h):
            return values[:, half(h)].rearrange("p (g j) -> p g j", j=GROUP)

        terms = tile("terms", [P, I], F32)
        neg_s = [tile("neg_s%d" % h, [P, 1], F32) for h in range(2)]
        for h in range(2):
            nc.vector.scalar_tensor_tensor(by_group(terms, h), c0[h], neg_inv_z[:], by_group(p_t, h),
                                           ALU.mult, ALU.mult, accum_out=neg_s[h][:])

        centred = tile("centred", [P, I], F32)
        partly = tile("partly", [P, HALF], F32)
        nc.scalar.activation(by_group(partly, 0), c0[0], ACT.Identity, bias=neg_s[0][:])
        nc.scalar.activation(centred[:, half(0)], partly[:], ACT.Identity, bias=neg_s[1][:])
        nc.vector.tensor_scalar(by_group(centred, 1), c0[1], neg_s[0][:], neg_s[1][:], ALU.add, ALU.add)
        nc.vector.tensor_tensor(gf[:].indirect(offsets[:]), centred[:], gain[:], ALU.mult)

        first = 0
        for n, width in enumerate(PIECES):
            cols = slice(first, first + width)
            piece = tile("piece%d" % n, [P, width], F32)
            nc.vector.tensor_tensor(piece[:], old_t[:, cols], gf[:, cols], ALU.add)
            nc.sync.dma_start(out[:, cols], piece[:])
            first = first + width
